import numpy as np
import ml_dtypes


def mxq(x, axis, fmt="e4m3"):
    dtype, down = {"e4m3": (ml_dtypes.float8_e4m3fn, 7), "e5m2": (ml_dtypes.float8_e5m2, 14)}[fmt]
    v = np.moveaxis(np.asarray(x, np.float32).astype(ml_dtypes.bfloat16).astype(np.float64), axis, -1)
    blocks = v.reshape(v.shape[:-1] + (-1, 32))
    amax = np.abs(blocks).max(-1, keepdims=True)
    byte = np.maximum(np.where(amax > 0, np.frexp(amax)[1] - 1 + 127, 0) - down, 1)
    scale = np.exp2(byte - 127.0)
    codes = (blocks / scale).astype(np.float32).astype(dtype).astype(np.float64)
    return np.moveaxis((codes * scale).reshape(v.shape), -1, axis)


WIDE = False


def mx_kscale(k):
    if not WIDE:
        return np.ones(k)
    levels = np.array([10, -10, 5, -5, 0])
    if k % 512:
        return np.exp2(np.random.permutation(np.resize(levels, k // 32))).repeat(32)
    a = np.empty((k // 512, 16))
    for p in range(k // 512):
        a[p, :8] = np.random.permutation(np.resize(levels, 8))
        for g in range(8):
            far = levels[np.abs(levels - a[p, g]) >= 10]
            a[p, g + 8] = far[np.random.randint(len(far))]
    return np.exp2(a.ravel()).repeat(32)


def f64(x):
    return np.asarray(x).astype(np.float64)


def split(x):
    m, e = np.frexp(f64(x))
    hi = np.ldexp(np.trunc(16.0 * m) / 16.0, e)
    return hi, f64(x) - hi


K, M, T = 2048, 512, 1024


def setup_inputs():
    n = np.random.standard_normal
    s = mx_kscale(K)[:, None]
    return {
        "w": (n((K, M)) / np.sqrt(K) / s).astype(np.float32),
        "x": (n((K, T)) * s).astype(np.float32),
    }


def reference(w, x):
    w_hi, w_lo = split(w)
    w_hi_, w_lo_ = mxq(w_hi, 0, "e4m3"), mxq(w_lo, 0, "e4m3")
    x_ = mxq(f64(x), 0, "e4m3")
    y = x_.T @ w_hi_ + x_.T @ w_lo_
    return y

@@ -1,0 +1,149 @@
+from contextlib import ExitStack
+
+import concourse.mybir as mybir
+
+K, N, T = 2048, 512, 1024
+FLOPS = 2 * 2 * K * N * T
+
+F32 = mybir.dt.float32
+BF16 = mybir.dt.bfloat16
+I32 = mybir.dt.int32
+U32 = mybir.dt.uint32
+U8 = mybir.dt.uint8
+FP8X4 = mybir.dt.float8_e4m3fn_x4
+ALU = mybir.AluOpType
+
+P = 128
+PACK = 4
+K_PASS = P * PACK
+PASSES = K // K_PASS
+PAIR = 256
+HALF_N = N // 2
+HI_MASK_F32 = -1048576
+HI_MASK_BF16_PAIR = -983056
+
+LOADS = ["w0a","w0b","w1","x0:0123","w2","x1:0123","w3","x2:01","x3:01","x2:23","x3:23"]
+ORDER = """
+M0a H0a U0a M0b H0b U0b H1 QL0 QH0 M1 QH1 U1 C01 C02 X01 C03 PH01 H2 QL1 PL01 X03 C00 PH03
+X02 PL03 X00 PH00 M2 PL00 U2 PL02 PH02 C13 C12 C10 X13 C11 PL13 H3 X10 PH13 QH2 PH10 QL2
+PL10 X12 X11 PH12 C21 C20 PH11 M3 PL11 X21 PH21 QH3 X20 PL12 U3 C30 PH20 PL20 C31 PL21 X30
+X31 PH30 C23 QL3 PH31 PL31 C22 X23 PL23 E11 PL30 X22 C33 PH22 E00 PL22 E10 C32 PH23 X33
+E01 PH33 X32 PL33 PH32 E31 E30 PL32 E21
+E20
+"""
+ROUTE = "ATTT"
+ON_VECTOR = "c00 c03 c11 c12 c21 e00 e01 e10 e11 e21 e31".split()
+
+
+def tile_mix_hilo_tm_none_kernel(tc, w, x, out):
+    nc = tc.nc
+
+    with ExitStack() as ctx:
+        keep = ctx.enter_context(tc.tile_pool(name="keep", bufs=1))
+        psum = ctx.enter_context(tc.psum_pool(name="psum", bufs=1))
+        ctx.enter_context(tc.manual_schedule())
+
+        w_raw, x_raw, w_hi_f32, grouped, codes, scales, results = {}, {}, {}, {}, {}, {}, {}
+        acc = [psum.tile([P, N], F32, name="acc%d" % i) for i in range(8)]
+        started, passes_done, evacuated = set(), {}, {}
+
+        def load_w(c, part):
+            n0, n1 = {"": (0, N), "a": (0, HALF_N), "b": (HALF_N, N)}[part]
+            t = keep.tile([P, PACK, n1 - n0], F32, name="w_raw%d%s" % (c, part))
+            nc.sync.dma_start(out=t[:], in_=w[c * K_PASS : (c + 1) * K_PASS, n0:n1].rearrange("(p j) n -> p j n", j=PACK))
+            w_raw[c, part] = (t, n0, n1)
+
+        def load_x(c, q0, q1):
+            t0, t1 = q0 * PAIR, q1 * PAIR
+            t = keep.tile([P, PACK, t1 - t0], F32, name="x_raw%d%d" % (c, q0))
+            nc.sync.dma_start(out=t[:], in_=x[c * K_PASS : (c + 1) * K_PASS, t0:t1].rearrange("(p j) t -> p j t", j=PACK))
+            for q in range(q0, q1):
+                x_raw[c, q] = t[:, :, (q - q0) * PAIR : (q - q0 + 1) * PAIR]
+
+        def w_group(which, c):
+            if (which, c) not in grouped:
+                grouped[which, c] = keep.tile([P, N, PACK], BF16, align_bytes=64, name="w_%s%d" % (which, c))
+            return grouped[which, c]
+
+        def pairs_in(ap):
+            return ap.rearrange("p j (g i) -> p g j i", i=2)
+
+        def pairs_out(which, c, n0, n1):
+            return w_group(which, c)[:, n0:n1, :].rearrange("p (g i) j -> p g j i", i=2)
+
+        def step_M(c, part):
+            t, n0, n1 = w_raw[c, part]
+            if ROUTE[c] == "A":
+                hi = keep.tile([P, PACK, n1 - n0], F32, name="w_hi_f32_%d%s" % (c, part))
+                nc.vector.tensor_scalar(
+                    out=hi[:].rearrange("p j n -> p (j n)").bitcast(I32),
+                    in0=t[:].rearrange("p j n -> p (j n)").bitcast(I32),
+                    scalar1=HI_MASK_F32, scalar2=None, op0=ALU.bitwise_and)
+                w_hi_f32[c, part] = hi
+            else:
+                words = w_group("hi", c)[:, n0:n1, :].rearrange("p n j -> p (n j)").bitcast(I32)
+                nc.vector.tensor_scalar(out=words, in0=words, scalar1=HI_MASK_BF16_PAIR, scalar2=None, op0=ALU.bitwise_and)
+
+        def step_H(c, part):
+            t, n0, n1 = w_raw[c, part]
+            src = w_hi_f32[c, part][:] if ROUTE[c] == "A" else t[:].bitcast(BF16)[:, :, 1::2]
+            nc.scalar.copy(out=pairs_out("hi", c, n0, n1), in_=pairs_in(src))
+
+        def step_U(c, part):
+            t, n0, n1 = w_raw[c, part]
+            hi = pairs_in(w_hi_f32[c, part][:]) if ROUTE[c] == "A" else pairs_out("hi", c, n0, n1)
+            nc.vector.tensor_tensor(out=pairs_out("lo", c, n0, n1), in0=pairs_in(t[:]), in1=hi, op=ALU.subtract)
+
+        def quantize(key, src, width):
+            label = "_".join(str(k) for k in key)
+            codes[key] = keep.tile([P, width], U32, align_bytes=64, name="codes_" + label)
+            scales[key] = keep.tile([P, width], U8, align_bytes=64, name="scales_" + label)
+            nc.vector.quantize_mx(out=codes[key][:].bitcast(FP8X4), scales=scales[key][:], in_=src)
+
+        def step_Q(which, c):
+            quantize((which, c), w_group(which, c)[:].rearrange("p n j -> p (n j)"), N)
+
+        def step_C(c, q):
+            t = keep.tile([P, 2, P, PACK], BF16, align_bytes=64, name="x_bf%d%d" % (c, q))
+            copy = nc.vector.tensor_copy if "c%d%d" % (c, q) in ON_VECTOR else nc.scalar.copy
+            copy(out=t[:].rearrange("p m g j -> p g j m"), in_=x_raw[c, q].rearrange("p j (g m) -> p g j m", m=2))
+            grouped["x", c, q] = t
+
+        def step_X(c, q):
+            quantize(("x", c, q), grouped["x", c, q][:].rearrange("p m g j -> p (m g j)"), PAIR)
+
+        def step_P(which, c, q):
+            for m in range(2):
+                b = 2 * q + m
+                cols = slice(m * P, (m + 1) * P)
+                passes_done[b] = passes_done.get(b, 0) + 1
+                nc.tensor.matmul_mx(
+                    out=acc[b][:],
+                    lhsT=codes["x", c, q][:, cols].bitcast(FP8X4), lhsT_scale=scales["x", c, q][:, cols],
+                    rhs=codes[which, c][:].bitcast(FP8X4), rhs_scale=scales[which, c][:],
+                    start=(passes_done[b] == 1), stop=(passes_done[b] == 2 * PASSES))
+
+        def step_E(q, m):
+            if q not in results:
+                results[q] = keep.tile([P, 2, N], F32, name="result%d" % q)
+            copy = nc.vector.tensor_copy if "e%d%d" % (q, m) in ON_VECTOR else nc.scalar.copy
+            copy(out=results[q][:, m, :], in_=acc[2 * q + m][:])
+            evacuated[q] = evacuated.get(q, 0) + 1
+            if evacuated[q] == 2:
+                rows = out[q * PAIR : (q + 1) * PAIR, :].rearrange("(p m) n -> p m n", m=2)
+                nc.sync.dma_start(out=rows, in_=results[q][:])
+
+        for name in LOADS:
+            if name[0] == "w":
+                load_w(int(name[1]), name[2:])
+            else:
+                load_x(int(name[1]), int(name[3]), int(name[-1]) + 1)
+        for step in ORDER.split():
+            if step[0] in "MHU":
+                {"M": step_M, "H": step_H, "U": step_U}[step[0]](int(step[1]), step[2:])
+            elif step[0] == "Q":
+                step_Q({"H": "hi", "L": "lo"}[step[1]], int(step[2]))
+            elif step[0] == "P":
+                step_P({"H": "hi", "L": "lo"}[step[1]], int(step[2]), int(step[3]))
+            else:
+                {"C": step_C, "X": step_X, "E": step_E}[step[0]](int(step[1]), int(step[2]))

@@ -66,10 +66,10 @@ def tile_mix_hilo_tm_none_kernel(tc, w, x, out):
             return grouped[which, c]
 
         def pairs_in(ap):
-            return ap.rearrange("p j (g i) -> p g j i", i=2)
+            return ap.rearrange("p j (g i) -> p g j i", i=4)
 
         def pairs_out(which, c, n0, n1):
-            return w_group(which, c)[:, n0:n1, :].rearrange("p (g i) j -> p g j i", i=2)
+            return w_group(which, c)[:, n0:n1, :].rearrange("p (g i) j -> p g j i", i=4)
 
         def step_M(c, part):
             t, n0, n1 = w_raw[c, part]
@@ -104,13 +104,13 @@ def tile_mix_hilo_tm_none_kernel(tc, w, x, out):
             quantize((which, c), w_group(which, c)[:].rearrange("p n j -> p (n j)"), N)
 
         def step_C(c, q):
-            t = keep.tile([P, 2, P, PACK], BF16, align_bytes=64, name="x_bf%d%d" % (c, q))
+            t = keep.tile([P, PAIR, PACK], BF16, align_bytes=64, name="x_bf%d%d" % (c, q))
             copy = nc.vector.tensor_copy if "c%d%d" % (c, q) in ON_VECTOR else nc.scalar.copy
-            copy(out=t[:].rearrange("p m g j -> p g j m"), in_=x_raw[c, q].rearrange("p j (g m) -> p g j m", m=2))
+            copy(out=t[:].rearrange("p (g i) j -> p g j i", i=4), in_=pairs_in(x_raw[c, q]))
             grouped["x", c, q] = t
 
         def step_X(c, q):
-            quantize(("x", c, q), grouped["x", c, q][:].rearrange("p m g j -> p (m g j)"), PAIR)
+            quantize(("x", c, q), grouped["x", c, q][:].rearrange("p t j -> p (t j)"), PAIR)
 
         def step_P(which, c, q):
             for m in range(2):
@@ -130,7 +130,7 @@ def tile_mix_hilo_tm_none_kernel(tc, w, x, out):
             copy(out=results[q][:, m, :], in_=acc[2 * q + m][:])
             evacuated[q] = evacuated.get(q, 0) + 1
             if evacuated[q] == 2:
-                rows = out[q * PAIR : (q + 1) * PAIR, :].rearrange("(p m) n -> p m n", m=2)
+                rows = out[q * PAIR : (q + 1) * PAIR, :].rearrange("(m p) n -> p m n", m=2)
                 nc.sync.dma_start(out=rows, in_=results[q][:])
 
         for name in LOADS:

@@ -17,22 +17,23 @@ P = 128
 PACK = 4
 K_PASS = P * PACK
 PASSES = K // K_PASS
-PAIR = 256
 HALF_N = N // 2
 HI_MASK_F32 = -1048576
 HI_MASK_BF16_PAIR = -983056
+W_PARTS = {"": (0, N), "a": (0, 256), "b": (256, N)}
 
-LOADS = ["w0a","w0b","w1","x0:0123","w2","x1:0123","w3","x2:01","x3:01","x2:23","x3:23"]
+LOADS = "w0a w2 w0b x2:0-7 w3 x0:0-7 x3:0-3 w1 x3:4-5 x1:0-3 x1:4-5 x3:6-7 x1:6-7".split()
 ORDER = """
-M0a H0a U0a M0b H0b U0b H1 QL0 QH0 M1 QH1 U1 C01 C02 X01 C03 PH01 H2 QL1 PL01 X03 C00 PH03
-X02 PL03 X00 PH00 M2 PL00 U2 PL02 PH02 C13 C12 C10 X13 C11 PL13 H3 X10 PH13 QH2 PH10 QL2
-PL10 X12 X11 PH12 C21 C20 PH11 M3 PL11 X21 PH21 QH3 X20 PL12 U3 C30 PH20 PL20 C31 PL21 X30
-X31 PH30 C23 QL3 PH31 PL31 C22 X23 PL23 E11 PL30 X22 C33 PH22 E00 PL22 E10 C32 PH23 X33
-E01 PH33 X32 PL33 PH32 E31 E30 PL32 E21
-E20
-"""
-ROUTE = "ATTT"
-ON_VECTOR = "c00 c03 c11 c12 c21 e00 e01 e10 e11 e21 e31".split()
+M0a H0a U0a M2 H2 M0b U2 H0b QH2 QL2 QH0 C20 U0b C26 X20 QL0 PH20 H3 PL20 C24 X26 C22 M3
+PH26 X24 PL26 X22 PL22 U3 PH24 PH22 C04 PL24 C06 C00 X04 X06 PH04 QH3 PL06 C33 C32 QL3
+PL04 C31 PH06 X32 X33 C30 X31 X00 PL32 C02 X30 PH00 H1 PL33 PL00 X02 PH30 C35 M1 PL02 C34
+X35 PH02 QH1 PL35 X34 PH34 U1 PL31 PH31 C10 PH33 PH32 PH35 PL34 C12 PL30 X10 QL1 PH10 C14
+PL10 X12 C37 PL12 F10 F00 PH12 X37 X14 F30 PL37 C16 PL14 F20 PH14 X16 C36 PH16 F50 PL16
+F40 PH37 X36 PH36 F70 PL36
+F60
+""".split()
+ROUTE = "ABAB"
+ON_VECTOR = "c06 c16 c32 c37 e10 e40 e50".split()
 
 
 def tile_mix_hilo_tm_none_kernel(tc, w, x, out):
@@ -45,36 +46,37 @@ def tile_mix_hilo_tm_none_kernel(tc, w, x, out):
 
         w_raw, x_raw, w_hi_f32, grouped, codes, scales, results = {}, {}, {}, {}, {}, {}, {}
         acc = [psum.tile([P, N], F32, name="acc%d" % i) for i in range(8)]
-        started, passes_done, evacuated = set(), {}, {}
+        passes_done, evacuated = {}, {}
+        engine_copy = {True: nc.vector.tensor_copy, False: nc.scalar.copy}
 
         def load_w(c, part):
-            n0, n1 = {"": (0, N), "a": (0, HALF_N), "b": (HALF_N, N)}[part]
+            n0, n1 = W_PARTS[part]
             t = keep.tile([P, PACK, n1 - n0], F32, name="w_raw%d%s" % (c, part))
             nc.sync.dma_start(out=t[:], in_=w[c * K_PASS : (c + 1) * K_PASS, n0:n1].rearrange("(p j) n -> p j n", j=PACK))
             w_raw[c, part] = (t, n0, n1)
 
         def load_x(c, q0, q1):
-            t0, t1 = q0 * PAIR, q1 * PAIR
-            t = keep.tile([P, PACK, t1 - t0], F32, name="x_raw%d%d" % (c, q0))
-            nc.sync.dma_start(out=t[:], in_=x[c * K_PASS : (c + 1) * K_PASS, t0:t1].rearrange("(p j) t -> p j t", j=PACK))
+            t = keep.tile([P, PACK, (q1 - q0) * P], F32, name="x_raw%d%d" % (c, q0))
+            rows = x[c * K_PASS : (c + 1) * K_PASS, q0 * P : q1 * P].rearrange("(p j) t -> p j t", j=PACK)
+            nc.sync.dma_start(out=t[:], in_=rows)
             for q in range(q0, q1):
-                x_raw[c, q] = t[:, :, (q - q0) * PAIR : (q - q0 + 1) * PAIR]
+                x_raw[c, q] = (t, (q - q0) * P)
 
         def w_group(which, c):
             if (which, c) not in grouped:
                 grouped[which, c] = keep.tile([P, N, PACK], BF16, align_bytes=64, name="w_%s%d" % (which, c))
             return grouped[which, c]
 
-        def pairs_in(ap):
+        def quads_in(ap):
             return ap.rearrange("p j (g i) -> p g j i", i=4)
 
-        def pairs_out(which, c, n0, n1):
-            return w_group(which, c)[:, n0:n1, :].rearrange("p (g i) j -> p g j i", i=4)
+        def quads_out(ap):
+            return ap.rearrange("p (g i) j -> p g j i", i=4)
 
         def step_M(c, part):
             t, n0, n1 = w_raw[c, part]
             if ROUTE[c] == "A":
-                hi = keep.tile([P, PACK, n1 - n0], F32, name="w_hi_f32_%d%s" % (c, part))
+                hi = keep.tile([P, PACK, n1 - n0], F32, name="w_hi_f32_%s" % (part or "full"))
                 nc.vector.tensor_scalar(
                     out=hi[:].rearrange("p j n -> p (j n)").bitcast(I32),
                     in0=t[:].rearrange("p j n -> p (j n)").bitcast(I32),
@@ -87,12 +89,12 @@ def tile_mix_hilo_tm_none_kernel(tc, w, x, out):
         def step_H(c, part):
             t, n0, n1 = w_raw[c, part]
             src = w_hi_f32[c, part][:] if ROUTE[c] == "A" else t[:].bitcast(BF16)[:, :, 1::2]
-            nc.scalar.copy(out=pairs_out("hi", c, n0, n1), in_=pairs_in(src))
+            engine_copy[ROUTE[c] == "B"](out=quads_out(w_group("hi", c)[:, n0:n1, :]), in_=quads_in(src))
 
         def step_U(c, part):
             t, n0, n1 = w_raw[c, part]
-            hi = pairs_in(w_hi_f32[c, part][:]) if ROUTE[c] == "A" else pairs_out("hi", c, n0, n1)
-            nc.vector.tensor_tensor(out=pairs_out("lo", c, n0, n1), in0=pairs_in(t[:]), in1=hi, op=ALU.subtract)
+            hi = quads_in(w_hi_f32[c, part][:]) if ROUTE[c] == "A" else quads_out(w_group("hi", c)[:, n0:n1, :])
+            nc.vector.tensor_tensor(out=quads_out(w_group("lo", c)[:, n0:n1, :]), in0=quads_in(t[:]), in1=hi, op=ALU.subtract)
 
         def quantize(key, src, width):
             label = "_".join(str(k) for k in key)
@@ -103,18 +105,22 @@ def tile_mix_hilo_tm_none_kernel(tc, w, x, out):
         def step_Q(which, c):
             quantize((which, c), w_group(which, c)[:].rearrange("p n j -> p (n j)"), N)
 
+        def tiles_of(c, q):
+            return 1 if c == 3 else 2
+
         def step_C(c, q):
-            t = keep.tile([P, PAIR, PACK], BF16, align_bytes=64, name="x_bf%d%d" % (c, q))
-            copy = nc.vector.tensor_copy if "c%d%d" % (c, q) in ON_VECTOR else nc.scalar.copy
-            copy(out=t[:].rearrange("p (g i) j -> p g j i", i=4), in_=pairs_in(x_raw[c, q]))
+            width = tiles_of(c, q) * P
+            t = keep.tile([P, width, PACK], BF16, align_bytes=64, name="x_bf%d%d" % (c, q))
+            src, t0 = x_raw[c, q]
+            engine_copy["c%d%d" % (c, q) in ON_VECTOR](out=quads_out(t[:]), in_=quads_in(src[:, :, t0 : t0 + width]))
             grouped["x", c, q] = t
 
         def step_X(c, q):
-            quantize(("x", c, q), grouped["x", c, q][:].rearrange("p t j -> p (t j)"), PAIR)
+            quantize(("x", c, q), grouped["x", c, q][:].rearrange("p t j -> p (t j)"), tiles_of(c, q) * P)
 
         def step_P(which, c, q):
-            for m in range(2):
-                b = 2 * q + m
+            for m in range(tiles_of(c, q)):
+                b = q + m
                 cols = slice(m * P, (m + 1) * P)
                 passes_done[b] = passes_done.get(b, 0) + 1
                 nc.tensor.matmul_mx(
@@ -123,27 +129,29 @@ def tile_mix_hilo_tm_none_kernel(tc, w, x, out):
                     rhs=codes[which, c][:].bitcast(FP8X4), rhs_scale=scales[which, c][:],
                     start=(passes_done[b] == 1), stop=(passes_done[b] == 2 * PASSES))
 
-        def step_E(q, m):
+        def evacuate(q, n0, n1, on_vector):
             if q not in results:
-                results[q] = keep.tile([P, 2, N], F32, name="result%d" % q)
-            copy = nc.vector.tensor_copy if "e%d%d" % (q, m) in ON_VECTOR else nc.scalar.copy
-            copy(out=results[q][:, m, :], in_=acc[2 * q + m][:])
-            evacuated[q] = evacuated.get(q, 0) + 1
-            if evacuated[q] == 2:
-                rows = out[q * PAIR : (q + 1) * PAIR, :].rearrange("(m p) n -> p m n", m=2)
-                nc.sync.dma_start(out=rows, in_=results[q][:])
+                results[q] = keep.tile([P, N], F32, name="result%d" % q)
+            engine_copy[on_vector](out=results[q][:, n0:n1], in_=acc[q][:, n0:n1])
+            evacuated[q] = evacuated.get(q, 0) + n1 - n0
+            if evacuated[q] == N:
+                nc.sync.dma_start(out=out[q * P : (q + 1) * P, :], in_=results[q][:])
+
+        def step_F(q, m):
+            evacuate(q, 0, N, "e%d0" % q in ON_VECTOR)
 
         for name in LOADS:
             if name[0] == "w":
                 load_w(int(name[1]), name[2:])
             else:
                 load_x(int(name[1]), int(name[3]), int(name[-1]) + 1)
-        for step in ORDER.split():
+        steps = {"M": step_M, "H": step_H, "U": step_U, "C": step_C, "X": step_X, "F": step_F}
+        for step in ORDER:
             if step[0] in "MHU":
-                {"M": step_M, "H": step_H, "U": step_U}[step[0]](int(step[1]), step[2:])
+                steps[step[0]](int(step[1]), step[2:])
             elif step[0] == "Q":
                 step_Q({"H": "hi", "L": "lo"}[step[1]], int(step[2]))
             elif step[0] == "P":
                 step_P({"H": "hi", "L": "lo"}[step[1]], int(step[2]), int(step[3]))
             else:
-                {"C": step_C, "X": step_X, "E": step_E}[step[0]](int(step[1]), int(step[2]))
+                steps[step[0]](int(step[1]), int(step[2]))

@@ -22,18 +22,18 @@ HI_MASK_F32 = -1048576
 HI_MASK_BF16_PAIR = -983056
 W_PARTS = {"": (0, N), "a": (0, 256), "b": (256, N)}
 
-LOADS = "w0a w2 w0b x2:0-7 w3 x0:0-7 x3:0-3 w1 x3:4-5 x1:0-3 x1:4-5 x3:6-7 x1:6-7".split()
+LOADS = "w0a w0b w2 x0:0-7 w3 x2:0-7 w1 x3:0-3 x1:0-3 x3:6-7 x1:4-7 x3:4-4 x3:5-5".split()
 ORDER = """
-M0a H0a U0a M2 H2 M0b U2 H0b QH2 QL2 QH0 C20 U0b C26 X20 QL0 PH20 H3 PL20 C24 X26 C22 M3
-PH26 X24 PL26 X22 PL22 U3 PH24 PH22 C04 PL24 C06 C00 X04 X06 PH04 QH3 PL06 C33 C32 QL3
-PL04 C31 PH06 X32 X33 C30 X31 X00 PL32 C02 X30 PH00 H1 PL33 PL00 X02 PH30 C35 M1 PL02 C34
-X35 PH02 QH1 PL35 X34 PH34 U1 PL31 PH31 C10 PH33 PH32 PH35 PL34 C12 PL30 X10 QL1 PH10 C14
-PL10 X12 C37 PL12 F10 F00 PH12 X37 X14 F30 PL37 C16 PL14 F20 PH14 X16 C36 PH16 F50 PL16
-F40 PH37 X36 PH36 F70 PL36
-F60
+M0a H0a U0a M0b H0b U0b M2 QL0 H2 U2 QH0 QH2 C02 C00 QL2 C06 X00 X02 PL00 M3 PH02 PL02 X06
+H3 U3 PH06 PL06 PH00 C04 QL3 C22 X04 C20 PH04 QH3 PL04 C26 X22 X20 PH22 H1 PL20 C24 PH20
+X26 PL22 M1 PL26 X24 C30 C33 PH24 QH1 PH26 C32 X33 X30 PL33 C31 PL30 X32 PL32 X31 U1 PH31
+PH30 C12 PH33 PL31 PH32 PL24 C10 X12 QL1 PH12 C37 PL12 C36 X10 F20 PL10 F30 X37 PH10 C16
+PL37 F10 PH37 X36 X16 PH36 F00 C14 PL36 PL16 C35 C34 PH16 X14 X34 PL14 F70 F60 PL34 X35
+PH14 PH34 PL35 F40 PH35
+F50
 """.split()
-ROUTE = "ABAB"
-ON_VECTOR = "c06 c16 c32 c37 e10 e40 e50".split()
+ROUTE = "ABAA"
+ON_VECTOR = "c00 c04 c14 c16 c20 c31 c33 c34 c37 e20 e70".split()
 
 
 def tile_mix_hilo_tm_none_kernel(tc, w, x, out):

from contextlib import ExitStack

import concourse.mybir as mybir

K, N, T = 2048, 512, 1024
FLOPS = 2 * 2 * K * N * T

F32 = mybir.dt.float32
BF16 = mybir.dt.bfloat16
I32 = mybir.dt.int32
U32 = mybir.dt.uint32
U8 = mybir.dt.uint8
FP8X4 = mybir.dt.float8_e4m3fn_x4
ALU = mybir.AluOpType

P = 128
PACK = 4
K_PASS = P * PACK
PASSES = K // K_PASS
HALF_N = N // 2
HI_MASK_F32 = -1048576
HI_MASK_BF16_PAIR = -983056
W_PARTS = {"": (0, N), "a": (0, 256), "b": (256, N)}

LOADS = "w0a w0b w2 x0:0-7 w3 x2:0-7 w1 x3:0-3 x1:0-3 x3:6-7 x1:4-7 x3:4-4 x3:5-5".split()
ORDER = """
M0a H0a U0a M0b H0b U0b M2 QL0 H2 U2 QH0 QH2 C02 C00 QL2 C06 X00 X02 PL00 M3 PH02 PL02 X06
H3 U3 PH06 PL06 PH00 C04 QL3 C22 X04 C20 PH04 QH3 PL04 C26 X22 X20 PH22 H1 PL20 C24 PH20
X26 PL22 M1 PL26 X24 C30 C33 PH24 QH1 PH26 C32 X33 X30 PL33 C31 PL30 X32 PL32 X31 U1 PH31
PH30 C12 PH33 PL31 PH32 PL24 C10 X12 QL1 PH12 C37 PL12 C36 X10 F20 PL10 F30 X37 PH10 C16
PL37 F10 PH37 X36 X16 PH36 F00 C14 PL36 PL16 C35 C34 PH16 X14 X34 PL14 F70 F60 PL34 X35
PH14 PH34 PL35 F40 PH35
F50
""".split()
ROUTE = "ABAA"
ON_VECTOR = "c00 c04 c14 c16 c20 c31 c33 c34 c37 e20 e70".split()


def tile_mix_hilo_tm_none_kernel(tc, w, x, out):
    nc = tc.nc

    with ExitStack() as ctx:
        keep = ctx.enter_context(tc.tile_pool(name="keep", bufs=1))
        psum = ctx.enter_context(tc.psum_pool(name="psum", bufs=1))
        ctx.enter_context(tc.manual_schedule())

        w_raw, x_raw, w_hi_f32, grouped, codes, scales, results = {}, {}, {}, {}, {}, {}, {}
        acc = [psum.tile([P, N], F32, name="acc%d" % i) for i in range(8)]
        passes_done, evacuated = {}, {}
        engine_copy = {True: nc.vector.tensor_copy, False: nc.scalar.copy}

        def load_w(c, part):
            n0, n1 = W_PARTS[part]
            t = keep.tile([P, PACK, n1 - n0], F32, name="w_raw%d%s" % (c, part))
            nc.sync.dma_start(out=t[:], in_=w[c * K_PASS : (c + 1) * K_PASS, n0:n1].rearrange("(p j) n -> p j n", j=PACK))
            w_raw[c, part] = (t, n0, n1)

        def load_x(c, q0, q1):
            t = keep.tile([P, PACK, (q1 - q0) * P], F32, name="x_raw%d%d" % (c, q0))
            rows = x[c * K_PASS : (c + 1) * K_PASS, q0 * P : q1 * P].rearrange("(p j) t -> p j t", j=PACK)
            nc.sync.dma_start(out=t[:], in_=rows)
            for q in range(q0, q1):
                x_raw[c, q] = (t, (q - q0) * P)

        def w_group(which, c):
            if (which, c) not in grouped:
                grouped[which, c] = keep.tile([P, N, PACK], BF16, align_bytes=64, name="w_%s%d" % (which, c))
            return grouped[which, c]

        def quads_in(ap):
            return ap.rearrange("p j (g i) -> p g j i", i=4)

        def quads_out(ap):
            return ap.rearrange("p (g i) j -> p g j i", i=4)

        def step_M(c, part):
            t, n0, n1 = w_raw[c, part]
            if ROUTE[c] == "A":
                hi = keep.tile([P, PACK, n1 - n0], F32, name="w_hi_f32_%s" % (part or "full"))
                nc.vector.tensor_scalar(
                    out=hi[:].rearrange("p j n -> p (j n)").bitcast(I32),
                    in0=t[:].rearrange("p j n -> p (j n)").bitcast(I32),
                    scalar1=HI_MASK_F32, scalar2=None, op0=ALU.bitwise_and)
                w_hi_f32[c, part] = hi
            else:
                words = w_group("hi", c)[:, n0:n1, :].rearrange("p n j -> p (n j)").bitcast(I32)
                nc.vector.tensor_scalar(out=words, in0=words, scalar1=HI_MASK_BF16_PAIR, scalar2=None, op0=ALU.bitwise_and)

        def step_H(c, part):
            t, n0, n1 = w_raw[c, part]
            src = w_hi_f32[c, part][:] if ROUTE[c] == "A" else t[:].bitcast(BF16)[:, :, 1::2]
            engine_copy[ROUTE[c] == "B"](out=quads_out(w_group("hi", c)[:, n0:n1, :]), in_=quads_in(src))

        def step_U(c, part):
            t, n0, n1 = w_raw[c, part]
            hi = quads_in(w_hi_f32[c, part][:]) if ROUTE[c] == "A" else quads_out(w_group("hi", c)[:, n0:n1, :])
            nc.vector.tensor_tensor(out=quads_out(w_group("lo", c)[:, n0:n1, :]), in0=quads_in(t[:]), in1=hi, op=ALU.subtract)

        def quantize(key, src, width):
            label = "_".join(str(k) for k in key)
            codes[key] = keep.tile([P, width], U32, align_bytes=64, name="codes_" + label)
            scales[key] = keep.tile([P, width], U8, align_bytes=64, name="scales_" + label)
            nc.vector.quantize_mx(out=codes[key][:].bitcast(FP8X4), scales=scales[key][:], in_=src)

        def step_Q(which, c):
            quantize((which, c), w_group(which, c)[:].rearrange("p n j -> p (n j)"), N)

        def tiles_of(c, q):
            return 1 if c == 3 else 2

        def step_C(c, q):
            width = tiles_of(c, q) * P
            t = keep.tile([P, width, PACK], BF16, align_bytes=64, name="x_bf%d%d" % (c, q))
            src, t0 = x_raw[c, q]
            engine_copy["c%d%d" % (c, q) in ON_VECTOR](out=quads_out(t[:]), in_=quads_in(src[:, :, t0 : t0 + width]))
            grouped["x", c, q] = t

        def step_X(c, q):
            quantize(("x", c, q), grouped["x", c, q][:].rearrange("p t j -> p (t j)"), tiles_of(c, q) * P)

        def step_P(which, c, q):
            for m in range(tiles_of(c, q)):
                b = q + m
                cols = slice(m * P, (m + 1) * P)
                passes_done[b] = passes_done.get(b, 0) + 1
                nc.tensor.matmul_mx(
                    out=acc[b][:],
                    lhsT=codes["x", c, q][:, cols].bitcast(FP8X4), lhsT_scale=scales["x", c, q][:, cols],
                    rhs=codes[which, c][:].bitcast(FP8X4), rhs_scale=scales[which, c][:],
                    start=(passes_done[b] == 1), stop=(passes_done[b] == 2 * PASSES))

        def evacuate(q, n0, n1, on_vector):
            if q not in results:
                results[q] = keep.tile([P, N], F32, name="result%d" % q)
            engine_copy[on_vector](out=results[q][:, n0:n1], in_=acc[q][:, n0:n1])
            evacuated[q] = evacuated.get(q, 0) + n1 - n0
            if evacuated[q] == N:
                nc.sync.dma_start(out=out[q * P : (q + 1) * P, :], in_=results[q][:])

        def step_F(q, m):
            evacuate(q, 0, N, "e%d0" % q in ON_VECTOR)

        for name in LOADS:
            if name[0] == "w":
                load_w(int(name[1]), name[2:])
            else:
                load_x(int(name[1]), int(name[3]), int(name[-1]) + 1)
        steps = {"M": step_M, "H": step_H, "U": step_U, "C": step_C, "X": step_X, "F": step_F}
        for step in ORDER:
            if step[0] in "MHU":
                steps[step[0]](int(step[1]), step[2:])
            elif step[0] == "Q":
                step_Q({"H": "hi", "L": "lo"}[step[1]], int(step[2]))
            elif step[0] == "P":
                step_P({"H": "hi", "L": "lo"}[step[1]], int(step[2]), int(step[3]))
            else:
                steps[step[0]](int(step[1]), int(step[2]))
